import numpy as np
import ml_dtypes


def mxq(x, axis, fmt="e4m3"):
    dtype, down = {"e4m3": (ml_dtypes.float8_e4m3fn, 7), "e5m2": (ml_dtypes.float8_e5m2, 14)}[fmt]
    v = np.moveaxis(np.asarray(x, np.float32).astype(ml_dtypes.bfloat16).astype(np.float64), axis, -1)
    blocks = v.reshape(v.shape[:-1] + (-1, 32))
    amax = np.abs(blocks).max(-1, keepdims=True)
    byte = np.maximum(np.where(amax > 0, np.frexp(amax)[1] - 1 + 127, 0) - down, 1)
    scale = np.exp2(byte - 127.0)
    codes = (blocks / scale).astype(np.float32).astype(dtype).astype(np.float64)
    return np.moveaxis((codes * scale).reshape(v.shape), -1, axis)


WIDE = False


def mx_kscale(k):
    if not WIDE:
        return np.ones(k)
    levels = np.array([10, -10, 5, -5, 0])
    if k % 512:
        return np.exp2(np.random.permutation(np.resize(levels, k // 32))).repeat(32)
    a = np.empty((k // 512, 16))
    for p in range(k // 512):
        a[p, :8] = np.random.permutation(np.resize(levels, 8))
        for g in range(8):
            far = levels[np.abs(levels - a[p, g]) >= 10]
            a[p, g + 8] = far[np.random.randint(len(far))]
    return np.exp2(a.ravel()).repeat(32)


def f64(x):
    return np.asarray(x).astype(np.float64)


def striped(idx):
    return np.tile(idx.reshape(-1, 16).T, (8, 1)).astype(np.uint16)


def unstriped(offs):
    return offs[:16].T.reshape(-1).astype(np.int64)


def relu(v):
    return np.maximum(v, 0.0)


K, T, D, S, V, H, N = 512, 2048, 4, 1024, 512, 512, 512
P = 2 ** 7


def setup_inputs():
    n = np.random.standard_normal
    s = mx_kscale(K)[:, None]
    u = mx_kscale(H)
    q = np.random.permutation(S)
    return {
        "xT": (n((K, T)) * s).astype(np.float32),
        "w1": (n((K, H)) / np.sqrt(K) / s * u).astype(np.float32),
        "w2": (n((H, N)) / np.sqrt(H) / u[:, None]).astype(np.float32),
        "gate": np.tile(np.random.uniform(0.2, 1.0, (D, 1, V)) / np.sqrt(D), (1, P, 1)).astype(np.float32),
        "offs": striped(np.random.permutation(T)[:S]),
        "pos1": striped(q[:V]),
        "pos2": striped(q[V:]),
        "pos3": striped(np.random.permutation(S)[:V]),
        "pos4": striped(np.random.permutation(S)[:V]),
    }


def reference(xT, w1, w2, gate, offs, pos1, pos2, pos3, pos4):
    h = relu(mxq(f64(w1), 0, "e4m3").T @ mxq(f64(xT)[:, unstriped(offs)], 0, "e4m3"))
    z = sum(f64(gate)[d, :1] * h[:, unstriped(p)] for d, p in enumerate((pos1, pos2, pos3, pos4)))
    return mxq(f64(w2), 0, "e4m3").T @ mxq(z, 0, "e4m3")

@@ -1,0 +1,214 @@
+from contextlib import ExitStack
+
+import concourse.mybir as mybir
+from concourse.masks import make_identity
+
+F32 = mybir.dt.float32
+BF16 = mybir.dt.bfloat16
+U32 = mybir.dt.uint32
+U16 = mybir.dt.uint16
+U8 = mybir.dt.uint8
+FP8X4 = mybir.dt.float8_e4m3fn_x4
+COPY = mybir.ActivationFunctionType.Copy
+RELU = mybir.ActivationFunctionType.Relu
+MULT = mybir.AluOpType.mult
+
+P = 128
+K, T, D, S, V, H, N = 512, 2048, 4, 1024, 512, 512, 512
+FLOPS = 2 * S * K * H + 2 * V * H * N
+
+X_CHUNKS = ((0, 0, 1024), (0, 1024, 2048), (1, 0, 1024), (1, 1024, 1536), (1, 1536, 2048))
+S_SLICES = ((0, 256), (256, 512), (512, 768), (768, 1024))
+
+
+def tile_picked_sage_relu_e_kernel(tc, xT, w1, w2, gate, offs, pos1, pos2, pos3, pos4, out):
+    nc = tc.nc
+    with ExitStack() as ctx:
+        keep = ctx.enter_context(tc.tile_pool(name="keep", bufs=1))
+        ring = ctx.enter_context(tc.tile_pool(name="ring", bufs=10))
+        banks = ctx.enter_context(tc.psum_pool(name="banks", bufs=8))
+
+        ident = keep.tile([P, P], F32, name="ident", align_bytes=64)
+        make_identity(nc, ident[:])
+        warm = keep.tile([P, 1], F32, name="warm")
+        nc.vector.memset(warm[:], 0.0)
+        nc.scalar.activation(warm[:], warm[:], RELU)
+
+        raw = [keep.tile([P, 2, T], F32, name=f"raw{u}") for u in range(2)]
+        x_view = xT.rearrange("(p j) t -> p j t", j=4)
+        offs_t = keep.tile([P, S // 16], U16, name="offs_t")
+        pos_t = [keep.tile([P, V // 16], U16, name=f"pos_t{d}") for d in range(D)]
+
+        def load_x(u, a, b):
+            nc.sync.dma_start(out=raw[u][:, :, a:b], in_=x_view[:, 2 * u : 2 * u + 2, a:b])
+
+        nc.sync.dma_start(offs_t[:], offs)
+        for c in X_CHUNKS:
+            load_x(*c)
+        w1_raw = keep.tile([P, 4, H], F32, name="w1_raw")
+        w1_view = w1.rearrange("(p j) i -> p j i", j=4)
+        for a in (0, 256):
+            nc.sync.dma_start(out=w1_raw[:, :, a : a + 256], in_=w1_view[:, :, a : a + 256])
+        for d, pos in enumerate((pos1, pos2, pos3, pos4)):
+            nc.sync.dma_start(pos_t[d][:], pos)
+        gate_t = [keep.tile([P, V], F32, name=f"gate_t{d}") for d in range(D)]
+        for d in range(D):
+            nc.sync.dma_start(out=gate_t[d][:], in_=gate[d])
+        w2_raw = keep.tile([P, 4, N], F32, name="w2_raw")
+        nc.sync.dma_start(out=w2_raw[:], in_=w2.rearrange("(p j) m -> p j m", j=4))
+
+        pairs = [keep.tile([P, T, 2], BF16, name=f"pairs{u}", align_bytes=64) for u in range(2)]
+        for u, a, b in X_CHUNKS:
+            mid = (a + b) // 2
+            nc.scalar.copy(pairs[u][:, a:mid, :], raw[u][:, :, a:mid].rearrange("p e t -> p t e"))
+            nc.vector.tensor_copy(pairs[u][:, mid:b, :], raw[u][:, :, mid:b].rearrange("p e t -> p t e"))
+        windows = [pairs[u][:].rearrange("p t e -> p (t e)").bitcast(U32) for u in range(2)]
+
+        xg = {a: keep.tile([P, 4 * (b - a)], BF16, name=f"xg{a}", align_bytes=64) for a, b in S_SLICES}
+        x_codes = keep.tile([P, S], U32, name="x_codes", align_bytes=64)
+        x_scales = keep.tile([P, S], U8, name="x_scales", align_bytes=64)
+
+        def gather_x(u, a, b):
+            words = xg[a][:].bitcast(U32).rearrange("p (n u) -> p n u", u=2)
+            nc.vector.tensor_copy(words[:, :, u], windows[u].indirect(offs_t[:, a // 16 : b // 16]))
+
+        for a, b in S_SLICES:
+            gather_x(0, a, b)
+
+        w1_grp = keep.tile([P, H, 4], BF16, name="w1_grp", align_bytes=64)
+        w1_codes = keep.tile([P, H], U32, name="w1_codes", align_bytes=64)
+        w1_scales = keep.tile([P, H], U8, name="w1_scales", align_bytes=64)
+        w2_grp = keep.tile([P, N, 4], BF16, name="w2_grp", align_bytes=64)
+        w2_codes = keep.tile([P, N], U32, name="w2_codes", align_bytes=64)
+        w2_scales = keep.tile([P, N], U8, name="w2_scales", align_bytes=64)
+
+        def cast_w(grp, rawt, a, b):
+            nc.scalar.copy(grp[:, a:b, :], rawt[:, :, a:b].rearrange("p j i -> p i j"))
+
+        def quant(codes, scales, grp, a, b):
+            nc.vector.quantize_mx(
+                out=codes[:, a:b].bitcast(FP8X4), scales=scales[:, a:b], in_=grp[:, 4 * a : 4 * b]
+            )
+
+        def quant_x(a, b):
+            nc.vector.quantize_mx(out=x_codes[:, a:b].bitcast(FP8X4), scales=x_scales[:, a:b], in_=xg[a][:])
+
+        w1_flat = w1_grp[:].rearrange("p i j -> p (i j)")
+        w2_flat = w2_grp[:].rearrange("p i j -> p (i j)")
+        for b in range(4):
+            cast_w(w1_grp, w1_raw, 128 * b, 128 * b + 128)
+        gather_x(1, 0, 256)
+        gather_x(1, 256, 512)
+        quant_x(0, 256)
+        quant(w1_codes, w1_scales, w1_flat, 0, 128)
+        gather_x(1, 512, 768)
+        quant_x(256, 512)
+        gather_x(1, 768, 1024)
+        quant_x(512, 768)
+        quant_x(768, 1024)
+
+        h_t = [keep.tile([P, S], F32, name=f"h_t{b}") for b in range(4)]
+
+        def layer1(b):
+            for lo, hi in S_SLICES if b == 0 else ((0, 512), (512, 1024)):
+                acc = banks.tile([P, 512], F32, name="bank")
+                nc.tensor.matmul_mx(
+                    out=acc[:, 0 : hi - lo],
+                    lhsT=w1_codes[:, 128 * b : 128 * b + 128].bitcast(FP8X4),
+                    lhsT_scale=w1_scales[:, 128 * b : 128 * b + 128],
+                    rhs=x_codes[:, lo:hi].bitcast(FP8X4),
+                    rhs_scale=x_scales[:, lo:hi],
+                    start=True,
+                    stop=True,
+                )
+                if b == 0 and lo == 768:
+                    nc.scalar.activation(h_t[b][:, lo : lo + 128], acc[:, 0:128], RELU)
+                    nc.vector.tensor_scalar_max(h_t[b][:, lo + 128 : hi], acc[:, 128:256], 0.0)
+                else:
+                    nc.scalar.activation(h_t[b][:, lo:hi], acc[:, 0 : hi - lo], RELU)
+
+        layer1(0)
+        quant(w1_codes, w1_scales, w1_flat, 128, 256)
+        quant(w1_codes, w1_scales, w1_flat, 256, 512)
+        for b in range(1, 4):
+            layer1(b)
+        for b in range(4):
+            cast_w(w2_grp, w2_raw, 128 * b, 128 * b + 128)
+
+        z_t = keep.tile([P, 4, H], BF16, name="z_t", align_bytes=64)
+
+        def gather(b, d, lo, hi):
+            g = ring.tile([P, 512], F32, name="g")
+            nc.vector.tensor_tensor(
+                g[:, 0 : hi - lo], h_t[b][:].indirect(pos_t[d][:, lo // 16 : hi // 16]), gate_t[d][:, lo:hi], MULT
+            )
+            return g
+
+        def add_transposed(dst, g, col, d):
+            nc.tensor.matmul(
+                dst, g[:, col : col + 128], ident[:], start=(d == 0), stop=(d == D - 1), is_transpose=True
+            )
+
+        def z_sums(b, lo, hi, last_cuts):
+            accs = {}
+            for vb in range(lo // 128, hi // 128):
+                accs[vb] = banks.tile([P, 512], F32, name="bank")
+            for d in range(D):
+                for a, e in last_cuts if d == D - 1 else ((lo, hi),):
+                    g = gather(b, d, a, e)
+                    for vb in range(a // 128, e // 128):
+                        add_transposed(accs[vb][:, 0:128], g, 128 * vb - a, d)
+            return accs
+
+        for b in range(3):
+            accs = z_sums(b, 0, 512, ((0, 512),))
+            for vb in range(4):
+                nc.scalar.copy(z_t[:, vb, 128 * b : 128 * b + 128], accs[vb][:, 0:128])
+
+        words_z = z_t[:].rearrange("p a i -> p (a i)").bitcast(F32).rearrange("p (a w) -> p a w", a=4)
+        zi = keep.tile([P, V * 4], BF16, name="zi", align_bytes=64)
+        zi_words = zi[:].bitcast(F32).rearrange("p (v u) -> p v u", u=2)
+        z_codes = keep.tile([P, V], U32, name="z_codes", align_bytes=64)
+        z_scales = keep.tile([P, V], U8, name="z_scales", align_bytes=64)
+
+        def turn(vb, acc, engine_copy):
+            engine_copy(z_t[:, vb, 384:512], acc[:, 0:128])
+            back = banks.tile([P, 512], F32, name="bank")
+            for u in range(2):
+                nc.tensor.transpose(back[:, 128 * u : 128 * u + 128], words_z[:, vb, u::2], ident[:])
+            engine_copy(zi_words[:, 128 * vb : 128 * vb + 128, :], back[:, 0:256].rearrange("p (u v) -> p v u", u=2))
+
+        o_view = out.rearrange("(a p) v -> p a v", p=P)
+
+        def layer2(lo, hi, copies, queues):
+            n = hi - lo
+            for half in range(2):
+                o_t = keep.tile([P, 2, n], F32, name=f"o_t{lo}_{half}")
+                acc = banks.tile([P, 512], F32, name="bank")
+                for q in range(2):
+                    m = 2 * half + q
+                    nc.tensor.matmul_mx(
+                        out=acc[:, q * n : q * n + n],
+                        lhsT=w2_codes[:, 128 * m : 128 * m + 128].bitcast(FP8X4),
+                        lhsT_scale=w2_scales[:, 128 * m : 128 * m + 128],
+                        rhs=z_codes[:, lo:hi].bitcast(FP8X4),
+                        rhs_scale=z_scales[:, lo:hi],
+                        start=True,
+                        stop=True,
+                    )
+                copies[half](o_t[:], acc[:, 0 : 2 * n].rearrange("p (a v) -> p a v", a=2))
+                queues[half].dma_start(out=o_view[:, 2 * half : 2 * half + 2, lo:hi], in_=o_t[:])
+
+        accs = z_sums(3, 0, 256, ((0, 256),))
+        for vb in range(2):
+            turn(vb, accs[vb], nc.scalar.copy)
+        accs = z_sums(3, 256, 512, ((256, 384), (384, 512)))
+        turn(2, accs[2], nc.scalar.copy)
+        turn(3, accs[3], nc.scalar.copy)
+        quant(w2_codes, w2_scales, w2_flat, 0, 512)
+        quant(z_codes, z_scales, zi, 0, 256)
+        layer2(0, 256, (nc.vector.tensor_copy, nc.scalar.copy), (nc.sync, nc.sync))
+        quant(z_codes, z_scales, zi, 256, 384)
+        layer2(256, 384, (nc.scalar.copy, nc.vector.tensor_copy), (nc.sync, nc.sync))
+        quant(z_codes, z_scales, zi, 384, 512)
+        layer2(384, 512, (nc.scalar.copy, nc.vector.tensor_copy), (nc.sync, nc.scalar))

@@ -42,17 +42,17 @@ def tile_picked_sage_relu_e_kernel(tc, xT, w1, w2, gate, offs, pos1, pos2, pos3,
         def load_x(u, a, b):
             nc.sync.dma_start(out=raw[u][:, :, a:b], in_=x_view[:, 2 * u : 2 * u + 2, a:b])
 
-        nc.sync.dma_start(offs_t[:], offs)
-        for c in X_CHUNKS:
+        for n, c in enumerate(X_CHUNKS):
             load_x(*c)
+            if n == 1:
+                nc.sync.dma_start(offs_t[:], offs)
         w1_raw = keep.tile([P, 4, H], F32, name="w1_raw")
         w1_view = w1.rearrange("(p j) i -> p j i", j=4)
-        for a in (0, 256):
-            nc.sync.dma_start(out=w1_raw[:, :, a : a + 256], in_=w1_view[:, :, a : a + 256])
+        for a, b in ((0, 128), (128, 512)):
+            nc.sync.dma_start(out=w1_raw[:, :, a:b], in_=w1_view[:, :, a:b])
+        gate_t = [keep.tile([P, V], F32, name=f"gate_t{d}") for d in range(D)]
         for d, pos in enumerate((pos1, pos2, pos3, pos4)):
             nc.sync.dma_start(pos_t[d][:], pos)
-        gate_t = [keep.tile([P, V], F32, name=f"gate_t{d}") for d in range(D)]
-        for d in range(D):
             nc.sync.dma_start(out=gate_t[d][:], in_=gate[d])
         w2_raw = keep.tile([P, 4, N], F32, name="w2_raw")
         nc.sync.dma_start(out=w2_raw[:], in_=w2.rearrange("(p j) m -> p j m", j=4))
@@ -75,7 +75,6 @@ def tile_picked_sage_relu_e_kernel(tc, xT, w1, w2, gate, offs, pos1, pos2, pos3,
         for a, b in S_SLICES:
             gather_x(0, a, b)
 
-        w1_grp = keep.tile([P, H, 4], BF16, name="w1_grp", align_bytes=64)
         w1_codes = keep.tile([P, H], U32, name="w1_codes", align_bytes=64)
         w1_scales = keep.tile([P, H], U8, name="w1_scales", align_bytes=64)
         w2_grp = keep.tile([P, N, 4], BF16, name="w2_grp", align_bytes=64)
@@ -93,14 +92,27 @@ def tile_picked_sage_relu_e_kernel(tc, xT, w1, w2, gate, offs, pos1, pos2, pos3,
         def quant_x(a, b):
             nc.vector.quantize_mx(out=x_codes[:, a:b].bitcast(FP8X4), scales=x_scales[:, a:b], in_=xg[a][:])
 
-        w1_flat = w1_grp[:].rearrange("p i j -> p (i j)")
+        def cast_w1(b):
+            grp = keep.tile([P, 128, 4], BF16, name="w1_first" if b == 0 else "w1_next", align_bytes=64)
+            cols = slice(128 * b, 128 * b + 128)
+            nc.scalar.copy(grp[:], w1_raw[:, :, cols].rearrange("p j i -> p i j"))
+            return grp
+
+        def quant_w1(b, grp):
+            cols = slice(128 * b, 128 * b + 128)
+            nc.vector.quantize_mx(
+                out=w1_codes[:, cols].bitcast(FP8X4),
+                scales=w1_scales[:, cols],
+                in_=grp[:].rearrange("p i j -> p (i j)"),
+            )
+
         w2_flat = w2_grp[:].rearrange("p i j -> p (i j)")
-        for b in range(4):
-            cast_w(w1_grp, w1_raw, 128 * b, 128 * b + 128)
+        w1_0 = cast_w1(0)
+        w1_1 = cast_w1(1)
         gather_x(1, 0, 256)
         gather_x(1, 256, 512)
         quant_x(0, 256)
-        quant(w1_codes, w1_scales, w1_flat, 0, 128)
+        quant_w1(0, w1_0)
         gather_x(1, 512, 768)
         quant_x(256, 512)
         gather_x(1, 768, 1024)
@@ -122,18 +134,11 @@ def tile_picked_sage_relu_e_kernel(tc, xT, w1, w2, gate, offs, pos1, pos2, pos3,
                     stop=True,
                 )
                 if b == 0 and lo == 768:
-                    nc.scalar.activation(h_t[b][:, lo : lo + 128], acc[:, 0:128], RELU)
-                    nc.vector.tensor_scalar_max(h_t[b][:, lo + 128 : hi], acc[:, 128:256], 0.0)
+                    nc.vector.tensor_scalar_max(h_t[b][:, lo:hi], acc[:, 0 : hi - lo], 0.0)
                 else:
                     nc.scalar.activation(h_t[b][:, lo:hi], acc[:, 0 : hi - lo], RELU)
 
         layer1(0)
-        quant(w1_codes, w1_scales, w1_flat, 128, 256)
-        quant(w1_codes, w1_scales, w1_flat, 256, 512)
-        for b in range(1, 4):
-            layer1(b)
-        for b in range(4):
-            cast_w(w2_grp, w2_raw, 128 * b, 128 * b + 128)
 
         z_t = keep.tile([P, 4, H], BF16, name="z_t", align_bytes=64)
 
@@ -149,7 +154,10 @@ def tile_picked_sage_relu_e_kernel(tc, xT, w1, w2, gate, offs, pos1, pos2, pos3,
                 dst, g[:, col : col + 128], ident[:], start=(d == 0), stop=(d == D - 1), is_transpose=True
             )
 
-        def z_sums(b, lo, hi, last_cuts):
+        def nothing():
+            pass
+
+        def z_sums(b, lo, hi, last_cuts, between=nothing):
             accs = {}
             for vb in range(lo // 128, hi // 128):
                 accs[vb] = banks.tile([P, 512], F32, name="bank")
@@ -158,12 +166,24 @@ def tile_picked_sage_relu_e_kernel(tc, xT, w1, w2, gate, offs, pos1, pos2, pos3,
                     g = gather(b, d, a, e)
                     for vb in range(a // 128, e // 128):
                         add_transposed(accs[vb][:, 0:128], g, 128 * vb - a, d)
+                if d == 1:
+                    between()
             return accs
 
+        def second_block():
+            quant_w1(1, w1_1)
+            layer1(1)
+
         for b in range(3):
-            accs = z_sums(b, 0, 512, ((0, 512),))
+            accs = z_sums(b, 0, 512, ((0, 512),), second_block if b == 0 else nothing)
             for vb in range(4):
                 nc.scalar.copy(z_t[:, vb, 128 * b : 128 * b + 128], accs[vb][:, 0:128])
+            if b == 0:
+                for later in (2, 3):
+                    quant_w1(later, cast_w1(later))
+                    layer1(later)
+                for c in range(4):
+                    cast_w(w2_grp, w2_raw, 128 * c, 128 * c + 128)
 
         words_z = z_t[:].rearrange("p a i -> p (a i)").bitcast(F32).rearrange("p (a w) -> p a w", a=4)
         zi = keep.tile([P, V * 4], BF16, name="zi", align_bytes=64)

from contextlib import ExitStack

import concourse.mybir as mybir
from concourse.masks import make_identity

F32 = mybir.dt.float32
BF16 = mybir.dt.bfloat16
U32 = mybir.dt.uint32
U16 = mybir.dt.uint16
U8 = mybir.dt.uint8
FP8X4 = mybir.dt.float8_e4m3fn_x4
COPY = mybir.ActivationFunctionType.Copy
RELU = mybir.ActivationFunctionType.Relu
MULT = mybir.AluOpType.mult

P = 128
K, T, D, S, V, H, N = 512, 2048, 4, 1024, 512, 512, 512
FLOPS = 2 * S * K * H + 2 * V * H * N

X_CHUNKS = ((0, 0, 1024), (0, 1024, 2048), (1, 0, 1024), (1, 1024, 1536), (1, 1536, 2048))
S_SLICES = ((0, 256), (256, 512), (512, 768), (768, 1024))


def tile_picked_sage_relu_e_kernel(tc, xT, w1, w2, gate, offs, pos1, pos2, pos3, pos4, out):
    nc = tc.nc
    with ExitStack() as ctx:
        keep = ctx.enter_context(tc.tile_pool(name="keep", bufs=1))
        ring = ctx.enter_context(tc.tile_pool(name="ring", bufs=10))
        banks = ctx.enter_context(tc.psum_pool(name="banks", bufs=8))

        ident = keep.tile([P, P], F32, name="ident", align_bytes=64)
        make_identity(nc, ident[:])
        warm = keep.tile([P, 1], F32, name="warm")
        nc.vector.memset(warm[:], 0.0)
        nc.scalar.activation(warm[:], warm[:], RELU)

        raw = [keep.tile([P, 2, T], F32, name=f"raw{u}") for u in range(2)]
        x_view = xT.rearrange("(p j) t -> p j t", j=4)
        offs_t = keep.tile([P, S // 16], U16, name="offs_t")
        pos_t = [keep.tile([P, V // 16], U16, name=f"pos_t{d}") for d in range(D)]

        def load_x(u, a, b):
            nc.sync.dma_start(out=raw[u][:, :, a:b], in_=x_view[:, 2 * u : 2 * u + 2, a:b])

        for n, c in enumerate(X_CHUNKS):
            load_x(*c)
            if n == 1:
                nc.sync.dma_start(offs_t[:], offs)
        w1_raw = keep.tile([P, 4, H], F32, name="w1_raw")
        w1_view = w1.rearrange("(p j) i -> p j i", j=4)
        for a, b in ((0, 128), (128, 512)):
            nc.sync.dma_start(out=w1_raw[:, :, a:b], in_=w1_view[:, :, a:b])
        gate_t = [keep.tile([P, V], F32, name=f"gate_t{d}") for d in range(D)]
        for d, pos in enumerate((pos1, pos2, pos3, pos4)):
            nc.sync.dma_start(pos_t[d][:], pos)
            nc.sync.dma_start(out=gate_t[d][:], in_=gate[d])
        w2_raw = keep.tile([P, 4, N], F32, name="w2_raw")
        nc.sync.dma_start(out=w2_raw[:], in_=w2.rearrange("(p j) m -> p j m", j=4))

        pairs = [keep.tile([P, T, 2], BF16, name=f"pairs{u}", align_bytes=64) for u in range(2)]
        for u, a, b in X_CHUNKS:
            mid = (a + b) // 2
            nc.scalar.copy(pairs[u][:, a:mid, :], raw[u][:, :, a:mid].rearrange("p e t -> p t e"))
            nc.vector.tensor_copy(pairs[u][:, mid:b, :], raw[u][:, :, mid:b].rearrange("p e t -> p t e"))
        windows = [pairs[u][:].rearrange("p t e -> p (t e)").bitcast(U32) for u in range(2)]

        xg = {a: keep.tile([P, 4 * (b - a)], BF16, name=f"xg{a}", align_bytes=64) for a, b in S_SLICES}
        x_codes = keep.tile([P, S], U32, name="x_codes", align_bytes=64)
        x_scales = keep.tile([P, S], U8, name="x_scales", align_bytes=64)

        def gather_x(u, a, b):
            words = xg[a][:].bitcast(U32).rearrange("p (n u) -> p n u", u=2)
            nc.vector.tensor_copy(words[:, :, u], windows[u].indirect(offs_t[:, a // 16 : b // 16]))

        for a, b in S_SLICES:
            gather_x(0, a, b)

        w1_codes = keep.tile([P, H], U32, name="w1_codes", align_bytes=64)
        w1_scales = keep.tile([P, H], U8, name="w1_scales", align_bytes=64)
        w2_grp = keep.tile([P, N, 4], BF16, name="w2_grp", align_bytes=64)
        w2_codes = keep.tile([P, N], U32, name="w2_codes", align_bytes=64)
        w2_scales = keep.tile([P, N], U8, name="w2_scales", align_bytes=64)

        def cast_w(grp, rawt, a, b):
            nc.scalar.copy(grp[:, a:b, :], rawt[:, :, a:b].rearrange("p j i -> p i j"))

        def quant(codes, scales, grp, a, b):
            nc.vector.quantize_mx(
                out=codes[:, a:b].bitcast(FP8X4), scales=scales[:, a:b], in_=grp[:, 4 * a : 4 * b]
            )

        def quant_x(a, b):
            nc.vector.quantize_mx(out=x_codes[:, a:b].bitcast(FP8X4), scales=x_scales[:, a:b], in_=xg[a][:])

        def cast_w1(b):
            grp = keep.tile([P, 128, 4], BF16, name="w1_first" if b == 0 else "w1_next", align_bytes=64)
            cols = slice(128 * b, 128 * b + 128)
            nc.scalar.copy(grp[:], w1_raw[:, :, cols].rearrange("p j i -> p i j"))
            return grp

        def quant_w1(b, grp):
            cols = slice(128 * b, 128 * b + 128)
            nc.vector.quantize_mx(
                out=w1_codes[:, cols].bitcast(FP8X4),
                scales=w1_scales[:, cols],
                in_=grp[:].rearrange("p i j -> p (i j)"),
            )

        w2_flat = w2_grp[:].rearrange("p i j -> p (i j)")
        w1_0 = cast_w1(0)
        w1_1 = cast_w1(1)
        gather_x(1, 0, 256)
        gather_x(1, 256, 512)
        quant_x(0, 256)
        quant_w1(0, w1_0)
        gather_x(1, 512, 768)
        quant_x(256, 512)
        gather_x(1, 768, 1024)
        quant_x(512, 768)
        quant_x(768, 1024)

        h_t = [keep.tile([P, S], F32, name=f"h_t{b}") for b in range(4)]

        def layer1(b):
            for lo, hi in S_SLICES if b == 0 else ((0, 512), (512, 1024)):
                acc = banks.tile([P, 512], F32, name="bank")
                nc.tensor.matmul_mx(
                    out=acc[:, 0 : hi - lo],
                    lhsT=w1_codes[:, 128 * b : 128 * b + 128].bitcast(FP8X4),
                    lhsT_scale=w1_scales[:, 128 * b : 128 * b + 128],
                    rhs=x_codes[:, lo:hi].bitcast(FP8X4),
                    rhs_scale=x_scales[:, lo:hi],
                    start=True,
                    stop=True,
                )
                if b == 0 and lo == 768:
                    nc.vector.tensor_scalar_max(h_t[b][:, lo:hi], acc[:, 0 : hi - lo], 0.0)
                else:
                    nc.scalar.activation(h_t[b][:, lo:hi], acc[:, 0 : hi - lo], RELU)

        layer1(0)

        z_t = keep.tile([P, 4, H], BF16, name="z_t", align_bytes=64)

        def gather(b, d, lo, hi):
            g = ring.tile([P, 512], F32, name="g")
            nc.vector.tensor_tensor(
                g[:, 0 : hi - lo], h_t[b][:].indirect(pos_t[d][:, lo // 16 : hi // 16]), gate_t[d][:, lo:hi], MULT
            )
            return g

        def add_transposed(dst, g, col, d):
            nc.tensor.matmul(
                dst, g[:, col : col + 128], ident[:], start=(d == 0), stop=(d == D - 1), is_transpose=True
            )

        def nothing():
            pass

        def z_sums(b, lo, hi, last_cuts, between=nothing):
            accs = {}
            for vb in range(lo // 128, hi // 128):
                accs[vb] = banks.tile([P, 512], F32, name="bank")
            for d in range(D):
                for a, e in last_cuts if d == D - 1 else ((lo, hi),):
                    g = gather(b, d, a, e)
                    for vb in range(a // 128, e // 128):
                        add_transposed(accs[vb][:, 0:128], g, 128 * vb - a, d)
                if d == 1:
                    between()
            return accs

        def second_block():
            quant_w1(1, w1_1)
            layer1(1)

        for b in range(3):
            accs = z_sums(b, 0, 512, ((0, 512),), second_block if b == 0 else nothing)
            for vb in range(4):
                nc.scalar.copy(z_t[:, vb, 128 * b : 128 * b + 128], accs[vb][:, 0:128])
            if b == 0:
                for later in (2, 3):
                    quant_w1(later, cast_w1(later))
                    layer1(later)
                for c in range(4):
                    cast_w(w2_grp, w2_raw, 128 * c, 128 * c + 128)

        words_z = z_t[:].rearrange("p a i -> p (a i)").bitcast(F32).rearrange("p (a w) -> p a w", a=4)
        zi = keep.tile([P, V * 4], BF16, name="zi", align_bytes=64)
        zi_words = zi[:].bitcast(F32).rearrange("p (v u) -> p v u", u=2)
        z_codes = keep.tile([P, V], U32, name="z_codes", align_bytes=64)
        z_scales = keep.tile([P, V], U8, name="z_scales", align_bytes=64)

        def turn(vb, acc, engine_copy):
            engine_copy(z_t[:, vb, 384:512], acc[:, 0:128])
            back = banks.tile([P, 512], F32, name="bank")
            for u in range(2):
                nc.tensor.transpose(back[:, 128 * u : 128 * u + 128], words_z[:, vb, u::2], ident[:])
            engine_copy(zi_words[:, 128 * vb : 128 * vb + 128, :], back[:, 0:256].rearrange("p (u v) -> p v u", u=2))

        o_view = out.rearrange("(a p) v -> p a v", p=P)

        def layer2(lo, hi, copies, queues):
            n = hi - lo
            for half in range(2):
                o_t = keep.tile([P, 2, n], F32, name=f"o_t{lo}_{half}")
                acc = banks.tile([P, 512], F32, name="bank")
                for q in range(2):
                    m = 2 * half + q
                    nc.tensor.matmul_mx(
                        out=acc[:, q * n : q * n + n],
                        lhsT=w2_codes[:, 128 * m : 128 * m + 128].bitcast(FP8X4),
                        lhsT_scale=w2_scales[:, 128 * m : 128 * m + 128],
                        rhs=z_codes[:, lo:hi].bitcast(FP8X4),
                        rhs_scale=z_scales[:, lo:hi],
                        start=True,
                        stop=True,
                    )
                copies[half](o_t[:], acc[:, 0 : 2 * n].rearrange("p (a v) -> p a v", a=2))
                queues[half].dma_start(out=o_view[:, 2 * half : 2 * half + 2, lo:hi], in_=o_t[:])

        accs = z_sums(3, 0, 256, ((0, 256),))
        for vb in range(2):
            turn(vb, accs[vb], nc.scalar.copy)
        accs = z_sums(3, 256, 512, ((256, 384), (384, 512)))
        turn(2, accs[2], nc.scalar.copy)
        turn(3, accs[3], nc.scalar.copy)
        quant(w2_codes, w2_scales, w2_flat, 0, 512)
        quant(z_codes, z_scales, zi, 0, 256)
        layer2(0, 256, (nc.vector.tensor_copy, nc.scalar.copy), (nc.sync, nc.sync))
        quant(z_codes, z_scales, zi, 256, 384)
        layer2(256, 384, (nc.scalar.copy, nc.vector.tensor_copy), (nc.sync, nc.sync))
        quant(z_codes, z_scales, zi, 384, 512)
        layer2(384, 512, (nc.scalar.copy, nc.vector.tensor_copy), (nc.sync, nc.scalar))
